import numpy as np
import ml_dtypes


def mxq(x, axis, fmt="e4m3"):
    dtype, down = {"e4m3": (ml_dtypes.float8_e4m3fn, 7), "e5m2": (ml_dtypes.float8_e5m2, 14)}[fmt]
    v = np.moveaxis(np.asarray(x, np.float32).astype(ml_dtypes.bfloat16).astype(np.float64), axis, -1)
    blocks = v.reshape(v.shape[:-1] + (-1, 32))
    amax = np.abs(blocks).max(-1, keepdims=True)
    byte = np.maximum(np.where(amax > 0, np.frexp(amax)[1] - 1 + 127, 0) - down, 1)
    scale = np.exp2(byte - 127.0)
    codes = (blocks / scale).astype(np.float32).astype(dtype).astype(np.float64)
    return np.moveaxis((codes * scale).reshape(v.shape), -1, axis)


WIDE = False


def mx_kscale(k):
    if not WIDE:
        return np.ones(k)
    levels = np.array([30, -30])
    if k % 512:
        return np.exp2(np.random.permutation(np.resize(levels, k // 32))).repeat(32)
    a = np.empty((k // 512, 16))
    for p in range(k // 512):
        a[p, :8] = np.random.permutation(np.resize(levels, 8))
        for g in range(8):
            far = levels[np.abs(levels - a[p, g]) >= 10]
            a[p, g + 8] = far[np.random.randint(len(far))]
    return np.exp2(a.ravel()).repeat(32)


def f64(x):
    return np.asarray(x).astype(np.float64)


def striped(idx):
    return np.tile(np.asarray(idx).reshape(-1, 16).T, (8, 1)).astype(np.uint16)


def unstriped(offs):
    return offs[:16].T.reshape(-1).astype(np.int64)


E2M1 = np.array([0.0, 0.5, 1.0, 1.5, 2.0, 3.0, 4.0, 6.0, -0.0, -0.5, -1.0, -1.5, -2.0, -3.0, -4.0, -6.0])


def pack_weight(w, fmt):
    k, n = w.shape
    w = f64(np.asarray(w, np.float32).astype(ml_dtypes.bfloat16)).reshape(k // 32, 32, n)
    amax = np.abs(w).max(1)
    if fmt in ("e4m3", "e5m2"):
        byte = np.frexp(amax)[1] - 1 + 127 - (7 if fmt == "e4m3" else 14)
    else:
        mant, ex = np.frexp(amax / 6.0)
        byte = np.where(mant > 0.5, ex, ex - 1) + 127
    byte = np.clip(np.where(amax > 0, byte, 1), 1, 254)
    scaled = (w * np.exp2(127.0 - byte)[:, None, :]).reshape(k, n).astype(np.float32)
    by_word = np.ascontiguousarray(scaled.reshape(k // 512, 128, 4, n).transpose(0, 1, 3, 2))
    if fmt in ("e4m3", "e5m2"):
        words = by_word.astype(ml_dtypes.float8_e4m3fn if fmt == "e4m3" else ml_dtypes.float8_e5m2).view(np.uint8)
    else:
        c = by_word.astype(ml_dtypes.float4_e2m1fn).view(np.uint8) & 0xF
        words = (c[..., 0::2] | (c[..., 1::2] << 4)).reshape(k // 512, 128, 2 * n)
    return np.ascontiguousarray(words), np.ascontiguousarray(byte.astype(np.uint8).reshape(k // 512, 16, n))


def unpack_weight(words, scales, fmt):
    g, _, n = scales.shape
    words = np.ascontiguousarray(words).reshape(g, 128, n, -1)
    if fmt in ("e4m3", "e5m2"):
        vals = words.view(ml_dtypes.float8_e4m3fn if fmt == "e4m3" else ml_dtypes.float8_e5m2).astype(np.float64)
    else:
        nib = np.empty((g, 128, n, 4), np.uint8)
        nib[..., 0::2] = words & 0xF
        nib[..., 1::2] = words >> 4
        vals = E2M1[nib]
    vals = vals * np.repeat(np.exp2(scales.astype(np.float64) - 127.0), 8, axis=1)[..., None]
    return vals.transpose(0, 1, 3, 2).reshape(g * 512, n)


K, F, T, Z, J, R, C, O, N = 512, 512, 1024, 1024, 256, 512, 512, 128, 256


def setup_inputs():
    n = np.random.standard_normal
    idx = np.random.permutation(T)[:J]
    idx2 = np.random.permutation(Z)[:J]
    idx3 = np.random.permutation(C)[:J]
    idx4 = np.random.permutation(C)[:O]
    idx5 = np.random.permutation(C)[:O]
    idx6 = np.random.permutation(T)[:O]
    fk = mx_kscale(K)
    fr = mx_kscale(R)
    ff = mx_kscale(F)
    xtp = pack_weight(n((K, T)) / fk[:, None], "e5m2")
    wp = pack_weight(n((K, R)) * 1 / np.sqrt(K) * fk[:, None] * fr, "e2m1")
    xop = pack_weight(n((F, Z)) / ff[:, None], "e4m3")
    w0p = pack_weight(n((F, R)) * 1 / np.sqrt(F) * ff[:, None] * fr, "e2m1")
    wbp = pack_weight(n((R, N)) * 1 / np.sqrt(R) / fr[:, None], "e2m1")
    wsp = pack_weight(n((K, N)) * 1 / np.sqrt(K) * fk[:, None], "e2m1")
    return {
        "xt_words": xtp[0],
        "xt_scales": xtp[1],
        "w_words": wp[0],
        "w_scales": wp[1],
        "xo_words": xop[0],
        "xo_scales": xop[1],
        "w0_words": w0p[0],
        "w0_scales": w0p[1],
        "wb_words": wbp[0],
        "wb_scales": wbp[1],
        "ws_words": wsp[0],
        "ws_scales": wsp[1],
        "offs": striped(idx),
        "offs2": striped(idx2),
        "offs3": striped(idx3),
        "offs4": striped(idx4),
        "offs5": striped(idx5),
        "offs6": striped(idx6),
    }


def reference(xt_words, xt_scales, w_words, w_scales, xo_words, xo_scales, w0_words, w0_scales, wb_words, wb_scales, ws_words, ws_scales, offs, offs2, offs3, offs4, offs5, offs6):
    idx = unstriped(offs)
    idx2 = unstriped(offs2)
    idx3 = unstriped(offs3)
    idx4 = unstriped(offs4)
    idx5 = unstriped(offs5)
    idx6 = unstriped(offs6)
    xtu = unpack_weight(xt_words, xt_scales, "e5m2")
    wu = unpack_weight(w_words, w_scales, "e2m1")
    xou = unpack_weight(xo_words, xo_scales, "e4m3")
    w0u = unpack_weight(w0_words, w0_scales, "e2m1")
    wbu = unpack_weight(wb_words, wb_scales, "e2m1")
    wsu = unpack_weight(ws_words, ws_scales, "e2m1")
    xtidxg = xtu[:, idx]
    xoidx2g = xou[:, idx2]
    a = wu.T @ xtidxg + w0u.T @ xoidx2g
    pw = np.zeros((R, C))
    pw[:, idx3] = a
    hid = np.maximum(pw[:, idx4], pw[:, idx5])
    hidq = mxq(hid, 0, "e4m3")
    xtidx6g = xtu[:, idx6]
    y = wbu.T @ hidq + wsu.T @ xtidx6g
    return y

@@ -1,0 +1,187 @@
+from contextlib import ExitStack
+
+import concourse.mybir as mybir
+
+K, T, Z, J, R, C, O, N = 512, 1024, 1024, 256, 512, 512, 128, 256
+FLOPS = 2 * (2 * K * R * J + 2 * K * N * O)
+
+F32 = mybir.dt.float32
+BF16 = mybir.dt.bfloat16
+I32 = mybir.dt.int32
+U32 = mybir.dt.uint32
+U16 = mybir.dt.uint16
+U8 = mybir.dt.uint8
+E4M3 = mybir.dt.float8_e4m3fn_x4
+E5M2 = mybir.dt.float8_e5m2_x4
+E2M1 = mybir.dt.float4_e2m1fn_x4
+COPY = mybir.ActivationFunctionType.Copy
+MAX = mybir.AluOpType.max
+
+P = 128
+PACK = 4
+
+
+def tile_list_readtwice_bank_further_plain_kernel(
+    tc, xt_words, xt_scales, w_words, w_scales, xo_words, xo_scales, w0_words, w0_scales,
+    wb_words, wb_scales, ws_words, ws_scales, offs, offs2, offs3, offs4, offs5, offs6, out,
+):
+    nc = tc.nc
+    with ExitStack() as ctx:
+        lists = ctx.enter_context(tc.tile_pool(name="lists", bufs=1))
+        sb = ctx.enter_context(tc.tile_pool(name="sb", bufs=1))
+        psum = ctx.enter_context(tc.psum_pool(name="psum", bufs=1))
+
+        def load_list(src, name):
+            tile = lists.tile(list(src.shape), U16, name=name)
+            nc.sync.dma_start(tile[:], src)
+            return tile
+
+        def load_table(src, name):
+            tile = sb.tile([P, src.shape[2]], U32, name=name, align_bytes=64)
+            nc.sync.dma_start(tile[:].bitcast(I32), src[0].rearrange("p n t -> p (n t)").bitcast(I32))
+            return tile
+
+        def load_weight(src, name):
+            tile = sb.tile([P, src.shape[2]], U8, name=name, align_bytes=64)
+            nc.sync.dma_start(tile[:].bitcast(I32), src[0].bitcast(I32))
+            return tile
+
+        def load_scales(src, name, queue_a, queue_b):
+            width = src.shape[2]
+            tile = sb.tile([P, width], U8, name=name, align_bytes=64)
+            rows = src[0].bitcast(I32)
+            dst = tile[:].bitcast(I32)
+            queue_b.dma_start(dst[0:16, :], rows)
+            queue_a.dma_start(dst[16:128, :], rows[2:16, :].unsqueeze(0).to_broadcast([8, 14, width // 4]))
+            return tile
+
+        def load_scales4(src, name, queue):
+            width = src.shape[2]
+            tile = sb.tile([P, width], U8, name=name, align_bytes=64)
+            rows = src[0].bitcast(I32)
+            dst = tile[:].bitcast(I32)
+            nc.vector.memset(dst, 0)
+            for q in range(4):
+                queue.dma_start(dst[32 * q : 32 * q + 4, :], rows[4 * q : 4 * q + 4, :])
+            return tile
+
+        l1 = load_list(offs, "l1")
+        xt_sc = load_scales(xt_scales, "xt_sc", nc.scalar, nc.sync)
+        xt = load_table(xt_words, "xt")
+        w_raw = load_weight(w_words, "w_raw")
+        w_sc_raw = load_scales(w_scales, "w_sc_raw", nc.scalar, nc.sync)
+        xo = load_table(xo_words, "xo")
+        xo_sc = load_scales(xo_scales, "xo_sc", nc.scalar, nc.sync)
+        l2 = load_list(offs2, "l2")
+        w0_raw = load_weight(w0_words, "w0_raw")
+        w0_sc_raw = load_scales(w0_scales, "w0_sc_raw", nc.sync, nc.sync)
+        l6 = load_list(offs6, "l6")
+        l3 = load_list(offs3, "l3")
+        l4 = load_list(offs4, "l4")
+        l5 = load_list(offs5, "l5")
+        ws = load_weight(ws_words, "ws")
+        ws_sc = load_scales(ws_scales, "ws_sc", nc.sync, nc.sync)
+        wb = load_weight(wb_words, "wb")
+        wb_sc = load_scales(wb_scales, "wb_sc", nc.sync, nc.sync)
+
+        boards = [sb.tile([P, C], F32, name="board%d" % t) for t in range(PACK)]
+        for board in boards:
+            nc.gpsimd.memset(board[:], 0.0)
+
+        def deal(raw, sc_raw, name):
+            words = sb.tile([P, 2 * R], U8, name=name, align_bytes=64)
+            scales = sb.tile([P, R], U8, name=name + "_sc", align_bytes=64)
+            nc.scalar.copy(
+                words[:].bitcast(U16).rearrange("p (t m) -> p t m", t=PACK),
+                raw[:].bitcast(U16).rearrange("p (m t) -> p t m", t=PACK),
+            )
+            nc.vector.tensor_copy(
+                scales[:].rearrange("p (t m) -> p t m", t=PACK),
+                sc_raw[:].rearrange("p (m t) -> p t m", t=PACK),
+            )
+            return words, scales
+
+        def pick(table, table_sc, offsets, count, name):
+            words = sb.tile([P, count], U32, name=name, align_bytes=64)
+            scales = sb.tile([P, count], U8, name=name + "_sc", align_bytes=64)
+            nc.vector.tensor_copy(words[:], table[:].indirect(offsets[:]))
+            nc.vector.tensor_copy(scales[:], table_sc[:].indirect(offsets[:]))
+            return words, scales
+
+        def mx(acc, weight, weight_sc, block, moving, moving_sc, fmt, start, stop):
+            nc.tensor.matmul_mx(
+                acc,
+                lhsT=weight[:, 2 * P * block : 2 * P * (block + 1)].bitcast(E2M1),
+                lhsT_scale=weight_sc[:, P * block : P * (block + 1)],
+                rhs=moving[:].bitcast(fmt),
+                rhs_scale=moving_sc[:],
+                start=start,
+                stop=stop,
+            )
+
+        w, w_sc = deal(w_raw, w_sc_raw, "w")
+        tok, tok_sc = pick(xt, xt_sc, l1, J, "tok")
+        w0, w0_sc = deal(w0_raw, w0_sc_raw, "w0")
+        note, note_sc = pick(xo, xo_sc, l2, J, "note")
+        short, short_sc = pick(xt, xt_sc, l6, O, "short")
+
+        accs = [psum.tile([P, J], F32, name="acc%d" % t) for t in range(PACK)]
+        for t in range(PACK):
+            mx(accs[t][:], w, w_sc, t, tok, tok_sc, E5M2, True, False)
+        for t in range(PACK):
+            mx(accs[t][:], w0, w0_sc, t, note, note_sc, E4M3, False, True)
+
+        ys = [psum.tile([P, O], F32, name="y%d" % h) for h in range(N // P)]
+        for h in range(N // P):
+            mx(ys[h][:], ws, ws_sc, h, short, short_sc, E5M2, True, False)
+
+        first = sb.tile([P, PACK, O], F32, name="first")
+        second = sb.tile([P, PACK, O], F32, name="second")
+        a = [sb.tile([P, J], F32, name="a%d" % t) for t in range(PACK)]
+
+        def place(t, on_scalar):
+            if on_scalar:
+                nc.scalar.activation(boards[t][:].indirect(l3[:]), a[t][:], COPY)
+            else:
+                nc.vector.tensor_copy(boards[t][:].indirect(l3[:]), a[t][:])
+
+        def read(t, on_scalar):
+            for dst, offsets in ((first, l4), (second, l5)):
+                if on_scalar:
+                    nc.scalar.activation(dst[:, t, :], boards[t][:].indirect(offsets[:]), COPY)
+                else:
+                    nc.vector.tensor_copy(dst[:, t, :], boards[t][:].indirect(offsets[:]))
+
+        nc.scalar.copy(a[0][:], accs[0][:])
+        nc.scalar.copy(a[1][:], accs[1][:])
+        place(0, False)
+        place(1, True)
+        nc.scalar.copy(a[2][:], accs[2][:])
+        nc.scalar.copy(a[3][:], accs[3][:])
+        read(0, False)
+        place(2, False)
+        place(3, True)
+        read(2, False)
+        read(1, True)
+        read(3, True)
+
+        hid = sb.tile([P, O * PACK], BF16, name="hid", align_bytes=64)
+        nc.vector.tensor_tensor(
+            hid[:].rearrange("p (c i t) -> p c t i", i=4, t=PACK),
+            first[:].rearrange("p t (c i) -> p c t i", i=4),
+            second[:].rearrange("p t (c i) -> p c t i", i=4),
+            MAX,
+        )
+        hq = sb.tile([P, O], U32, name="hq", align_bytes=64)
+        hq_sc = sb.tile([P, O], U8, name="hq_sc", align_bytes=64)
+        nc.vector.quantize_mx(out=hq[:].bitcast(E4M3), scales=hq_sc[:], in_=hid[:])
+
+        for h in range(N // P):
+            mx(ys[h][:], wb, wb_sc, h, hq, hq_sc, E4M3, False, True)
+            res = sb.tile([P, O], F32, name="res%d" % h)
+            if h == 0:
+                nc.scalar.copy(res[:], ys[h][:])
+                nc.scalar.dma_start(out[P * h : P * (h + 1), :], res[:])
+            else:
+                nc.vector.tensor_copy(res[:], ys[h][:])
+                nc.sync.dma_start(out[P * h : P * (h + 1), :], res[:])

@@ -19,6 +19,7 @@ MAX = mybir.AluOpType.max
 
 P = 128
 PACK = 4
+HALF = J // 2
 
 
 def tile_list_readtwice_bank_further_plain_kernel(
@@ -46,66 +47,73 @@ def tile_list_readtwice_bank_further_plain_kernel(
             nc.sync.dma_start(tile[:].bitcast(I32), src[0].bitcast(I32))
             return tile
 
-        def load_scales(src, name, queue_a, queue_b):
-            width = src.shape[2]
-            tile = sb.tile([P, width], U8, name=name, align_bytes=64)
-            rows = src[0].bitcast(I32)
-            dst = tile[:].bitcast(I32)
-            queue_b.dma_start(dst[0:16, :], rows)
-            queue_a.dma_start(dst[16:128, :], rows[2:16, :].unsqueeze(0).to_broadcast([8, 14, width // 4]))
-            return tile
+        def plane(src, name):
+            return sb.tile([P, src.shape[2]], U8, name=name, align_bytes=64)
 
-        def load_scales4(src, name, queue):
-            width = src.shape[2]
-            tile = sb.tile([P, width], U8, name=name, align_bytes=64)
-            rows = src[0].bitcast(I32)
-            dst = tile[:].bitcast(I32)
-            nc.vector.memset(dst, 0)
-            for q in range(4):
-                queue.dma_start(dst[32 * q : 32 * q + 4, :], rows[4 * q : 4 * q + 4, :])
-            return tile
+        def load_low(tile, src, queue):
+            queue.dma_start(tile[0:16, :].bitcast(I32), src[0].bitcast(I32))
 
+        def load_high(tile, src, queue):
+            rows = src[0].bitcast(I32)[2:16, :]
+            queue.dma_start(tile[16:128, :].bitcast(I32), rows.unsqueeze(0).to_broadcast([8, 14, rows.shape[1]]))
+
+        xt_sc = plane(xt_scales, "xt_sc")
+        xo_sc = plane(xo_scales, "xo_sc")
+        w_sc_raw = plane(w_scales, "w_sc_raw")
+        w0_sc_raw = plane(w0_scales, "w0_sc_raw")
+        ws_sc = plane(ws_scales, "ws_sc")
+        wb_sc = plane(wb_scales, "wb_sc")
         l1 = load_list(offs, "l1")
-        xt_sc = load_scales(xt_scales, "xt_sc", nc.scalar, nc.sync)
-        xt = load_table(xt_words, "xt")
+        load_high(xt_sc, xt_scales, nc.scalar)
+        load_low(xt_sc, xt_scales, nc.sync)
+        load_low(w_sc_raw, w_scales, nc.sync)
         w_raw = load_weight(w_words, "w_raw")
-        w_sc_raw = load_scales(w_scales, "w_sc_raw", nc.scalar, nc.sync)
-        xo = load_table(xo_words, "xo")
-        xo_sc = load_scales(xo_scales, "xo_sc", nc.scalar, nc.sync)
-        l2 = load_list(offs2, "l2")
+        xt = load_table(xt_words, "xt")
+        load_high(w_sc_raw, w_scales, nc.scalar)
         w0_raw = load_weight(w0_words, "w0_raw")
-        w0_sc_raw = load_scales(w0_scales, "w0_sc_raw", nc.sync, nc.sync)
+        xo = load_table(xo_words, "xo")
+        l2 = load_list(offs2, "l2")
+        load_high(xo_sc, xo_scales, nc.sync)
+        load_low(xo_sc, xo_scales, nc.sync)
+        load_high(w0_sc_raw, w0_scales, nc.sync)
+        load_low(w0_sc_raw, w0_scales, nc.sync)
         l6 = load_list(offs6, "l6")
         l3 = load_list(offs3, "l3")
         l4 = load_list(offs4, "l4")
         l5 = load_list(offs5, "l5")
         ws = load_weight(ws_words, "ws")
-        ws_sc = load_scales(ws_scales, "ws_sc", nc.sync, nc.sync)
+        load_high(ws_sc, ws_scales, nc.sync)
+        load_low(ws_sc, ws_scales, nc.sync)
         wb = load_weight(wb_words, "wb")
-        wb_sc = load_scales(wb_scales, "wb_sc", nc.sync, nc.sync)
+        load_high(wb_sc, wb_scales, nc.sync)
+        load_low(wb_sc, wb_scales, nc.sync)
 
         boards = [sb.tile([P, C], F32, name="board%d" % t) for t in range(PACK)]
         for board in boards:
             nc.gpsimd.memset(board[:], 0.0)
 
-        def deal(raw, sc_raw, name):
+        def deal_words(raw, name, copy):
             words = sb.tile([P, 2 * R], U8, name=name, align_bytes=64)
-            scales = sb.tile([P, R], U8, name=name + "_sc", align_bytes=64)
-            nc.scalar.copy(
+            copy(
                 words[:].bitcast(U16).rearrange("p (t m) -> p t m", t=PACK),
                 raw[:].bitcast(U16).rearrange("p (m t) -> p t m", t=PACK),
             )
+            return words
+
+        def deal_scales(sc_raw, name):
+            scales = sb.tile([P, R], U8, name=name, align_bytes=64)
             nc.vector.tensor_copy(
                 scales[:].rearrange("p (t m) -> p t m", t=PACK),
                 sc_raw[:].rearrange("p (m t) -> p t m", t=PACK),
             )
-            return words, scales
+            return scales
 
-        def pick(table, table_sc, offsets, count, name):
+        def pick(table, table_sc, offsets, name):
+            count = 16 * offsets.shape[1]
             words = sb.tile([P, count], U32, name=name, align_bytes=64)
             scales = sb.tile([P, count], U8, name=name + "_sc", align_bytes=64)
-            nc.vector.tensor_copy(words[:], table[:].indirect(offsets[:]))
-            nc.vector.tensor_copy(scales[:], table_sc[:].indirect(offsets[:]))
+            nc.vector.tensor_copy(words[:], table[:].indirect(offsets))
+            nc.vector.tensor_copy(scales[:], table_sc[:].indirect(offsets))
             return words, scales
 
         def mx(acc, weight, weight_sc, block, moving, moving_sc, fmt, start, stop):
@@ -113,57 +121,61 @@ def tile_list_readtwice_bank_further_plain_kernel(
                 acc,
                 lhsT=weight[:, 2 * P * block : 2 * P * (block + 1)].bitcast(E2M1),
                 lhsT_scale=weight_sc[:, P * block : P * (block + 1)],
-                rhs=moving[:].bitcast(fmt),
-                rhs_scale=moving_sc[:],
+                rhs=moving.bitcast(fmt),
+                rhs_scale=moving_sc,
                 start=start,
                 stop=stop,
             )
 
-        w, w_sc = deal(w_raw, w_sc_raw, "w")
-        tok, tok_sc = pick(xt, xt_sc, l1, J, "tok")
-        w0, w0_sc = deal(w0_raw, w0_sc_raw, "w0")
-        note, note_sc = pick(xo, xo_sc, l2, J, "note")
-        short, short_sc = pick(xt, xt_sc, l6, O, "short")
+        first = sb.tile([P, PACK, O], F32, name="first")
+        second = sb.tile([P, PACK, O], F32, name="second")
 
-        accs = [psum.tile([P, J], F32, name="acc%d" % t) for t in range(PACK)]
-        for t in range(PACK):
-            mx(accs[t][:], w, w_sc, t, tok, tok_sc, E5M2, True, False)
-        for t in range(PACK):
-            mx(accs[t][:], w0, w0_sc, t, note, note_sc, E4M3, False, True)
+        def place(t, offsets, values, on_scalar):
+            if on_scalar:
+                nc.scalar.activation(boards[t][:].indirect(offsets), values, COPY)
+            else:
+                nc.vector.tensor_copy(boards[t][:].indirect(offsets), values)
+
+        def read(t, dst, offsets, on_scalar):
+            if on_scalar:
+                nc.scalar.activation(dst[:, t, :], boards[t][:].indirect(offsets[:]), COPY)
+            else:
+                nc.vector.tensor_copy(dst[:, t, :], boards[t][:].indirect(offsets[:]))
+
+        w_sc = deal_scales(w_sc_raw, "w_sc")
+        tok, tok_sc = pick(xt, xt_sc, l1[:], "tok")
+        w = deal_words(w_raw, "w", nc.scalar.copy)
+        w0 = deal_words(w0_raw, "w0", nc.scalar.copy)
+        notes = [pick(xo, xo_sc, l2[:, 0:8], "note0")]
+        w0_sc = deal_scales(w0_sc_raw, "w0_sc")
+        notes.append(pick(xo, xo_sc, l2[:, 8:16], "note1"))
+        short, short_sc = pick(xt, xt_sc, l6[:], "short")
+
+        parts = [(0, 0), (0, 1), (1, 1), (1, 0)]
+        accs = {part: psum.tile([P, 2, HALF], F32, name="acc%d%d" % part) for part in parts}
+        for h, pair in parts:
+            cols = slice(HALF * h, HALF * (h + 1))
+            for u in range(2):
+                mx(accs[h, pair][:, u, :], w, w_sc, 2 * pair + u, tok[:, cols], tok_sc[:, cols], E5M2, u == 0, False)
+        for h, pair in parts:
+            for u in range(2):
+                mx(accs[h, pair][:, u, :], w0, w0_sc, 2 * pair + u, notes[h][0][:], notes[h][1][:], E4M3, False, u == 1)
 
         ys = [psum.tile([P, O], F32, name="y%d" % h) for h in range(N // P)]
         for h in range(N // P):
-            mx(ys[h][:], ws, ws_sc, h, short, short_sc, E5M2, True, False)
+            mx(ys[h][:], ws, ws_sc, h, short[:], short_sc[:], E5M2, True, False)
 
-        first = sb.tile([P, PACK, O], F32, name="first")
-        second = sb.tile([P, PACK, O], F32, name="second")
-        a = [sb.tile([P, J], F32, name="a%d" % t) for t in range(PACK)]
-
-        def place(t, on_scalar):
-            if on_scalar:
-                nc.scalar.activation(boards[t][:].indirect(l3[:]), a[t][:], COPY)
+        for h, pair in [(0, 0), (1, 1), (0, 1), (1, 0)]:
+            a = sb.tile([P, 2, HALF], F32, name="a%d%d" % (h, pair))
+            if h == 0:
+                nc.scalar.copy(a[:], accs[h, pair][:])
             else:
-                nc.vector.tensor_copy(boards[t][:].indirect(l3[:]), a[t][:])
-
-        def read(t, on_scalar):
-            for dst, offsets in ((first, l4), (second, l5)):
-                if on_scalar:
-                    nc.scalar.activation(dst[:, t, :], boards[t][:].indirect(offsets[:]), COPY)
-                else:
-                    nc.vector.tensor_copy(dst[:, t, :], boards[t][:].indirect(offsets[:]))
-
-        nc.scalar.copy(a[0][:], accs[0][:])
-        nc.scalar.copy(a[1][:], accs[1][:])
-        place(0, False)
-        place(1, True)
-        nc.scalar.copy(a[2][:], accs[2][:])
-        nc.scalar.copy(a[3][:], accs[3][:])
-        read(0, False)
-        place(2, False)
-        place(3, True)
-        read(2, False)
-        read(1, True)
-        read(3, True)
+                nc.vector.tensor_copy(a[:], accs[h, pair][:])
+            for u in range(2):
+                place(2 * pair + u, l3[:, 8 * h : 8 * h + 8], a[:, u, :], h == 0)
+        for t, on_scalar in [(2, True), (3, True), (0, True), (1, False)]:
+            read(t, first, l4, on_scalar)
+            read(t, second, l5, on_scalar and t != 0)
 
         hid = sb.tile([P, O * PACK], BF16, name="hid", align_bytes=64)
         nc.vector.tensor_tensor(
@@ -177,7 +189,7 @@ def tile_list_readtwice_bank_further_plain_kernel(
         nc.vector.quantize_mx(out=hq[:].bitcast(E4M3), scales=hq_sc[:], in_=hid[:])
 
         for h in range(N // P):
-            mx(ys[h][:], wb, wb_sc, h, hq, hq_sc, E4M3, False, True)
+            mx(ys[h][:], wb, wb_sc, h, hq[:], hq_sc[:], E4M3, False, True)
             res = sb.tile([P, O], F32, name="res%d" % h)
             if h == 0:
                 nc.scalar.copy(res[:], ys[h][:])

@@ -2,7 +2,7 @@ from contextlib import ExitStack
 
 import concourse.mybir as mybir
 
-K, T, Z, J, R, C, O, N = 512, 1024, 1024, 256, 512, 512, 128, 256
+K, J, R, C, O, N = 512, 256, 512, 512, 128, 256
 FLOPS = 2 * (2 * K * R * J + 2 * K * N * O)
 
 F32 = mybir.dt.float32
@@ -19,7 +19,12 @@ MAX = mybir.AluOpType.max
 
 P = 128
 PACK = 4
+QUADRANT = 32
+SCALE_ROWS = 16
+PERIOD = 14
 HALF = J // 2
+HALF_COLS = HALF // 16
+ALIGN = 64
 
 
 def tile_list_readtwice_bank_further_plain_kernel(
@@ -32,51 +37,62 @@ def tile_list_readtwice_bank_further_plain_kernel(
         sb = ctx.enter_context(tc.tile_pool(name="sb", bufs=1))
         psum = ctx.enter_context(tc.psum_pool(name="psum", bufs=1))
 
+
         def load_list(src, name):
             tile = lists.tile(list(src.shape), U16, name=name)
             nc.sync.dma_start(tile[:], src)
             return tile
 
         def load_table(src, name):
-            tile = sb.tile([P, src.shape[2]], U32, name=name, align_bytes=64)
+            tile = sb.tile([P, src.shape[2]], U32, name=name, align_bytes=ALIGN)
             nc.sync.dma_start(tile[:].bitcast(I32), src[0].rearrange("p n t -> p (n t)").bitcast(I32))
             return tile
 
         def load_weight(src, name):
-            tile = sb.tile([P, src.shape[2]], U8, name=name, align_bytes=64)
+            tile = sb.tile([P, src.shape[2]], U8, name=name, align_bytes=ALIGN)
             nc.sync.dma_start(tile[:].bitcast(I32), src[0].bitcast(I32))
             return tile
 
-        def plane(src, name):
-            return sb.tile([P, src.shape[2]], U8, name=name, align_bytes=64)
+        def new_plane(src, name):
+            return sb.tile([P, src.shape[2]], U8, name=name, align_bytes=ALIGN)
 
-        def load_low(tile, src, queue):
-            queue.dma_start(tile[0:16, :].bitcast(I32), src[0].bitcast(I32))
+        def load_quadrants(plane, src, queue):
+            for q in range(P // QUADRANT):
+                rows = src[0].bitcast(I32)[PACK * q : PACK * (q + 1), :]
+                queue.dma_start(plane[QUADRANT * q : QUADRANT * q + PACK, :].bitcast(I32), rows)
 
-        def load_high(tile, src, queue):
-            rows = src[0].bitcast(I32)[2:16, :]
-            queue.dma_start(tile[16:128, :].bitcast(I32), rows.unsqueeze(0).to_broadcast([8, 14, rows.shape[1]]))
+        def load_low(plane, src, queue):
+            queue.dma_start(plane[0:SCALE_ROWS, :].bitcast(I32), src[0].bitcast(I32))
 
-        xt_sc = plane(xt_scales, "xt_sc")
-        xo_sc = plane(xo_scales, "xo_sc")
-        w_sc_raw = plane(w_scales, "w_sc_raw")
-        w0_sc_raw = plane(w0_scales, "w0_sc_raw")
-        ws_sc = plane(ws_scales, "ws_sc")
-        wb_sc = plane(wb_scales, "wb_sc")
+        def load_high(plane, src, queue):
+            rows = src[0].bitcast(I32)[SCALE_ROWS - PERIOD :, :]
+            repeats = (P - SCALE_ROWS) // PERIOD
+            queue.dma_start(
+                plane[SCALE_ROWS:P, :].bitcast(I32),
+                rows.unsqueeze(0).to_broadcast([repeats, PERIOD, rows.shape[1]]),
+            )
+
+        xt_sc = new_plane(xt_scales, "xt_sc")
+        xo_sc = new_plane(xo_scales, "xo_sc")
+        w_sc_raw = new_plane(w_scales, "w_sc_raw")
+        w0_sc_raw = new_plane(w0_scales, "w0_sc_raw")
+        ws_sc = new_plane(ws_scales, "ws_sc")
+        wb_sc = new_plane(wb_scales, "wb_sc")
+
+        nc.gpsimd.memset(xt_sc[:].bitcast(I32), 0)
+        nc.vector.memset(xo_sc[:].bitcast(I32), 0)
+        load_low(w_sc_raw, w_scales, nc.gpsimd)
+        load_high(w0_sc_raw, w0_scales, nc.gpsimd)
         l1 = load_list(offs, "l1")
-        load_high(xt_sc, xt_scales, nc.scalar)
-        load_low(xt_sc, xt_scales, nc.sync)
-        load_low(w_sc_raw, w_scales, nc.sync)
+        load_quadrants(xt_sc, xt_scales, nc.scalar)
         w_raw = load_weight(w_words, "w_raw")
         xt = load_table(xt_words, "xt")
-        load_high(w_sc_raw, w_scales, nc.scalar)
-        w0_raw = load_weight(w0_words, "w0_raw")
+        load_high(w_sc_raw, w_scales, nc.sync)
         xo = load_table(xo_words, "xo")
         l2 = load_list(offs2, "l2")
-        load_high(xo_sc, xo_scales, nc.sync)
-        load_low(xo_sc, xo_scales, nc.sync)
-        load_high(w0_sc_raw, w0_scales, nc.sync)
         load_low(w0_sc_raw, w0_scales, nc.sync)
+        w0_raw = load_weight(w0_words, "w0_raw")
+        load_quadrants(xo_sc, xo_scales, nc.sync)
         l6 = load_list(offs6, "l6")
         l3 = load_list(offs3, "l3")
         l4 = load_list(offs4, "l4")
@@ -90,80 +106,66 @@ def tile_list_readtwice_bank_further_plain_kernel(
 
         boards = [sb.tile([P, C], F32, name="board%d" % t) for t in range(PACK)]
         for board in boards:
-            nc.gpsimd.memset(board[:], 0.0)
+            nc.vector.memset(board[:], 0.0)
 
-        def deal_words(raw, name, copy):
-            words = sb.tile([P, 2 * R], U8, name=name, align_bytes=64)
-            copy(
+        def deal_words(raw, name):
+            words = sb.tile([P, 2 * R], U8, name=name, align_bytes=ALIGN)
+            nc.scalar.copy(
                 words[:].bitcast(U16).rearrange("p (t m) -> p t m", t=PACK),
                 raw[:].bitcast(U16).rearrange("p (m t) -> p t m", t=PACK),
             )
             return words
 
-        def deal_scales(sc_raw, name):
-            scales = sb.tile([P, R], U8, name=name, align_bytes=64)
+        def deal_scales(raw, name):
+            scales = sb.tile([P, R], U8, name=name, align_bytes=ALIGN)
             nc.vector.tensor_copy(
                 scales[:].rearrange("p (t m) -> p t m", t=PACK),
-                sc_raw[:].rearrange("p (m t) -> p t m", t=PACK),
+                raw[:].rearrange("p (m t) -> p t m", t=PACK),
             )
             return scales
 
-        def pick(table, table_sc, offsets, name):
-            count = 16 * offsets.shape[1]
-            words = sb.tile([P, count], U32, name=name, align_bytes=64)
-            scales = sb.tile([P, count], U8, name=name + "_sc", align_bytes=64)
-            nc.vector.tensor_copy(words[:], table[:].indirect(offsets))
-            nc.vector.tensor_copy(scales[:], table_sc[:].indirect(offsets))
-            return words, scales
+        def gather(window, offsets, name, tag=None):
+            picked = sb.tile([P, P], window.dtype, name=name, tag=tag or name, align_bytes=ALIGN)
+            nc.vector.tensor_copy(picked[:], window[:].indirect(offsets))
+            return picked
+
+        def half(offsets, h):
+            return offsets[:, HALF_COLS * h : HALF_COLS * (h + 1)]
 
         def mx(acc, weight, weight_sc, block, moving, moving_sc, fmt, start, stop):
             nc.tensor.matmul_mx(
                 acc,
                 lhsT=weight[:, 2 * P * block : 2 * P * (block + 1)].bitcast(E2M1),
                 lhsT_scale=weight_sc[:, P * block : P * (block + 1)],
-                rhs=moving.bitcast(fmt),
-                rhs_scale=moving_sc,
+                rhs=moving[:].bitcast(fmt),
+                rhs_scale=moving_sc[:],
                 start=start,
                 stop=stop,
             )
 
-        first = sb.tile([P, PACK, O], F32, name="first")
-        second = sb.tile([P, PACK, O], F32, name="second")
-
-        def place(t, offsets, values, on_scalar):
-            if on_scalar:
-                nc.scalar.activation(boards[t][:].indirect(offsets), values, COPY)
-            else:
-                nc.vector.tensor_copy(boards[t][:].indirect(offsets), values)
-
-        def read(t, dst, offsets, on_scalar):
-            if on_scalar:
-                nc.scalar.activation(dst[:, t, :], boards[t][:].indirect(offsets[:]), COPY)
-            else:
-                nc.vector.tensor_copy(dst[:, t, :], boards[t][:].indirect(offsets[:]))
-
+        toks = [(gather(xt, half(l1, 0), "tok0"), gather(xt_sc, half(l1, 0), "tok0_sc"))]
         w_sc = deal_scales(w_sc_raw, "w_sc")
-        tok, tok_sc = pick(xt, xt_sc, l1[:], "tok")
-        w = deal_words(w_raw, "w", nc.scalar.copy)
-        w0 = deal_words(w0_raw, "w0", nc.scalar.copy)
-        notes = [pick(xo, xo_sc, l2[:, 0:8], "note0")]
+        toks.append((gather(xt, half(l1, 1), "tok1"), gather(xt_sc, half(l1, 1), "tok1_sc")))
+        w = deal_words(w_raw, "w")
+        w0 = deal_words(w0_raw, "w0")
+        note0 = gather(xo, half(l2, 0), "note0")
         w0_sc = deal_scales(w0_sc_raw, "w0_sc")
-        notes.append(pick(xo, xo_sc, l2[:, 8:16], "note1"))
-        short, short_sc = pick(xt, xt_sc, l6[:], "short")
+        notes = [(note0, gather(xo_sc, half(l2, 0), "note0_sc"))]
+        notes.append((gather(xo, half(l2, 1), "note1"), gather(xo_sc, half(l2, 1), "note1_sc")))
 
         parts = [(0, 0), (0, 1), (1, 1), (1, 0)]
         accs = {part: psum.tile([P, 2, HALF], F32, name="acc%d%d" % part) for part in parts}
         for h, pair in parts:
-            cols = slice(HALF * h, HALF * (h + 1))
             for u in range(2):
-                mx(accs[h, pair][:, u, :], w, w_sc, 2 * pair + u, tok[:, cols], tok_sc[:, cols], E5M2, u == 0, False)
+                mx(accs[h, pair][:, u, :], w, w_sc, 2 * pair + u, *toks[h], E5M2, u == 0, False)
         for h, pair in parts:
             for u in range(2):
-                mx(accs[h, pair][:, u, :], w0, w0_sc, 2 * pair + u, notes[h][0][:], notes[h][1][:], E4M3, False, u == 1)
+                mx(accs[h, pair][:, u, :], w0, w0_sc, 2 * pair + u, *notes[h], E4M3, False, u == 1)
 
-        ys = [psum.tile([P, O], F32, name="y%d" % h) for h in range(N // P)]
-        for h in range(N // P):
-            mx(ys[h][:], ws, ws_sc, h, short[:], short_sc[:], E5M2, True, False)
+        short = (gather(xt, l6[:], "short", "tok1"), gather(xt_sc, l6[:], "short_sc", "tok1_sc"))
+        ys = [psum.tile([P, O], F32, name="y%d" % block) for block in range(N // P)]
+        for block in range(N // P):
+            mx(ys[block][:], ws, ws_sc, block, *short, E5M2, True, False)
 
         for h, pair in [(0, 0), (1, 1), (0, 1), (1, 0)]:
             a = sb.tile([P, 2, HALF], F32, name="a%d%d" % (h, pair))
@@ -172,28 +174,45 @@ def tile_list_readtwice_bank_further_plain_kernel(
             else:
                 nc.vector.tensor_copy(a[:], accs[h, pair][:])
             for u in range(2):
-                place(2 * pair + u, l3[:, 8 * h : 8 * h + 8], a[:, u, :], h == 0)
-        for t, on_scalar in [(2, True), (3, True), (0, True), (1, False)]:
-            read(t, first, l4, on_scalar)
-            read(t, second, l5, on_scalar and t != 0)
+                columns = boards[2 * pair + u][:].indirect(half(l3, h))
+                if h == 0:
+                    nc.scalar.activation(columns, a[:, u, :], COPY)
+                else:
+                    nc.vector.tensor_copy(columns, a[:, u, :])
 
-        hid = sb.tile([P, O * PACK], BF16, name="hid", align_bytes=64)
-        nc.vector.tensor_tensor(
-            hid[:].rearrange("p (c i t) -> p c t i", i=4, t=PACK),
-            first[:].rearrange("p t (c i) -> p c t i", i=4),
-            second[:].rearrange("p t (c i) -> p c t i", i=4),
-            MAX,
-        )
-        hq = sb.tile([P, O], U32, name="hq", align_bytes=64)
-        hq_sc = sb.tile([P, O], U8, name="hq_sc", align_bytes=64)
+        first = [sb.tile([P, 2, O], F32, name="first%d" % pair) for pair in range(2)]
+        second = [sb.tile([P, 2, O], F32, name="second%d" % pair) for pair in range(2)]
+
+        def read_board(t, dst, offsets, on_scalar):
+            picked = dst[t // 2][:, t % 2, :]
+            if on_scalar:
+                nc.scalar.activation(picked, boards[t][:].indirect(offsets[:]), COPY)
+            else:
+                nc.vector.tensor_copy(picked, boards[t][:].indirect(offsets[:]))
+
+        for t in (2, 3, 0, 1):
+            read_board(t, first, l4, on_scalar=t != 1)
+            read_board(t, second, l5, on_scalar=t >= 2)
+
+        hid = sb.tile([P, O * PACK], BF16, name="hid", align_bytes=ALIGN)
+        for pair in (1, 0):
+            nc.vector.tensor_tensor(
+                hid[:].rearrange("p (c i t) -> p c t i", i=4, t=PACK)[:, :, 2 * pair : 2 * pair + 2, :],
+                first[pair][:].rearrange("p t (c i) -> p c t i", i=4),
+                second[pair][:].rearrange("p t (c i) -> p c t i", i=4),
+                MAX,
+            )
+        hq = sb.tile([P, O], U32, name="hq", align_bytes=ALIGN)
+        hq_sc = sb.tile([P, O], U8, name="hq_sc", align_bytes=ALIGN)
         nc.vector.quantize_mx(out=hq[:].bitcast(E4M3), scales=hq_sc[:], in_=hid[:])
 
-        for h in range(N // P):
-            mx(ys[h][:], wb, wb_sc, h, hq[:], hq_sc[:], E4M3, False, True)
-            res = sb.tile([P, O], F32, name="res%d" % h)
-            if h == 0:
-                nc.scalar.copy(res[:], ys[h][:])
-                nc.scalar.dma_start(out[P * h : P * (h + 1), :], res[:])
+        for block in range(N // P):
+            mx(ys[block][:], wb, wb_sc, block, hq, hq_sc, E4M3, False, True)
+            res = sb.tile([P, O], F32, name="res%d" % block)
+            rows = out[P * block : P * (block + 1), :]
+            if block == 0:
+                nc.scalar.copy(res[:], ys[block][:])
+                nc.scalar.dma_start(rows, res[:])
             else:
-                nc.vector.tensor_copy(res[:], ys[h][:])
-                nc.sync.dma_start(out[P * h : P * (h + 1), :], res[:])
+                nc.vector.tensor_copy(res[:], ys[block][:])
+                nc.sync.dma_start(rows, res[:])

@@ -105,8 +105,8 @@ def tile_list_readtwice_bank_further_plain_kernel(
         load_low(wb_sc, wb_scales, nc.sync)
 
         boards = [sb.tile([P, C], F32, name="board%d" % t) for t in range(PACK)]
-        for board in boards:
-            nc.vector.memset(board[:], 0.0)
+        for t, board in enumerate(boards):
+            (nc.gpsimd if t < 2 else nc.vector).memset(board[:], 0.0)
 
         def deal_words(raw, name):
             words = sb.tile([P, 2 * R], U8, name=name, align_bytes=ALIGN)
@@ -180,28 +180,23 @@ def tile_list_readtwice_bank_further_plain_kernel(
                 else:
                     nc.vector.tensor_copy(columns, a[:, u, :])
 
-        first = [sb.tile([P, 2, O], F32, name="first%d" % pair) for pair in range(2)]
-        second = [sb.tile([P, 2, O], F32, name="second%d" % pair) for pair in range(2)]
-
-        def read_board(t, dst, offsets, on_scalar):
-            picked = dst[t // 2][:, t % 2, :]
-            if on_scalar:
-                nc.scalar.activation(picked, boards[t][:].indirect(offsets[:]), COPY)
-            else:
-                nc.vector.tensor_copy(picked, boards[t][:].indirect(offsets[:]))
-
+        first = sb.tile([P, PACK, O], F32, name="first")
+        second = sb.tile([P, PACK, O], F32, name="second")
         for t in (2, 3, 0, 1):
-            read_board(t, first, l4, on_scalar=t != 1)
-            read_board(t, second, l5, on_scalar=t >= 2)
+            for picked, offsets in ((first, l4), (second, l5)):
+                columns = boards[t][:].indirect(offsets[:])
+                if t >= 2:
+                    nc.scalar.activation(picked[:, t, :], columns, COPY)
+                else:
+                    nc.vector.tensor_copy(picked[:, t, :], columns)
 
         hid = sb.tile([P, O * PACK], BF16, name="hid", align_bytes=ALIGN)
-        for pair in (1, 0):
-            nc.vector.tensor_tensor(
-                hid[:].rearrange("p (c i t) -> p c t i", i=4, t=PACK)[:, :, 2 * pair : 2 * pair + 2, :],
-                first[pair][:].rearrange("p t (c i) -> p c t i", i=4),
-                second[pair][:].rearrange("p t (c i) -> p c t i", i=4),
-                MAX,
-            )
+        nc.vector.tensor_tensor(
+            hid[:].rearrange("p (c i t) -> p c t i", i=4, t=PACK),
+            first[:].rearrange("p t (c i) -> p c t i", i=4),
+            second[:].rearrange("p t (c i) -> p c t i", i=4),
+            MAX,
+        )
         hq = sb.tile([P, O], U32, name="hq", align_bytes=ALIGN)
         hq_sc = sb.tile([P, O], U8, name="hq_sc", align_bytes=ALIGN)
         nc.vector.quantize_mx(out=hq[:].bitcast(E4M3), scales=hq_sc[:], in_=hid[:])

from contextlib import ExitStack

import concourse.mybir as mybir

K, J, R, C, O, N = 512, 256, 512, 512, 128, 256
FLOPS = 2 * (2 * K * R * J + 2 * K * N * O)

F32 = mybir.dt.float32
BF16 = mybir.dt.bfloat16
I32 = mybir.dt.int32
U32 = mybir.dt.uint32
U16 = mybir.dt.uint16
U8 = mybir.dt.uint8
E4M3 = mybir.dt.float8_e4m3fn_x4
E5M2 = mybir.dt.float8_e5m2_x4
E2M1 = mybir.dt.float4_e2m1fn_x4
COPY = mybir.ActivationFunctionType.Copy
MAX = mybir.AluOpType.max

P = 128
PACK = 4
QUADRANT = 32
SCALE_ROWS = 16
PERIOD = 14
HALF = J // 2
HALF_COLS = HALF // 16
ALIGN = 64


def tile_list_readtwice_bank_further_plain_kernel(
    tc, xt_words, xt_scales, w_words, w_scales, xo_words, xo_scales, w0_words, w0_scales,
    wb_words, wb_scales, ws_words, ws_scales, offs, offs2, offs3, offs4, offs5, offs6, out,
):
    nc = tc.nc
    with ExitStack() as ctx:
        lists = ctx.enter_context(tc.tile_pool(name="lists", bufs=1))
        sb = ctx.enter_context(tc.tile_pool(name="sb", bufs=1))
        psum = ctx.enter_context(tc.psum_pool(name="psum", bufs=1))


        def load_list(src, name):
            tile = lists.tile(list(src.shape), U16, name=name)
            nc.sync.dma_start(tile[:], src)
            return tile

        def load_table(src, name):
            tile = sb.tile([P, src.shape[2]], U32, name=name, align_bytes=ALIGN)
            nc.sync.dma_start(tile[:].bitcast(I32), src[0].rearrange("p n t -> p (n t)").bitcast(I32))
            return tile

        def load_weight(src, name):
            tile = sb.tile([P, src.shape[2]], U8, name=name, align_bytes=ALIGN)
            nc.sync.dma_start(tile[:].bitcast(I32), src[0].bitcast(I32))
            return tile

        def new_plane(src, name):
            return sb.tile([P, src.shape[2]], U8, name=name, align_bytes=ALIGN)

        def load_quadrants(plane, src, queue):
            for q in range(P // QUADRANT):
                rows = src[0].bitcast(I32)[PACK * q : PACK * (q + 1), :]
                queue.dma_start(plane[QUADRANT * q : QUADRANT * q + PACK, :].bitcast(I32), rows)

        def load_low(plane, src, queue):
            queue.dma_start(plane[0:SCALE_ROWS, :].bitcast(I32), src[0].bitcast(I32))

        def load_high(plane, src, queue):
            rows = src[0].bitcast(I32)[SCALE_ROWS - PERIOD :, :]
            repeats = (P - SCALE_ROWS) // PERIOD
            queue.dma_start(
                plane[SCALE_ROWS:P, :].bitcast(I32),
                rows.unsqueeze(0).to_broadcast([repeats, PERIOD, rows.shape[1]]),
            )

        xt_sc = new_plane(xt_scales, "xt_sc")
        xo_sc = new_plane(xo_scales, "xo_sc")
        w_sc_raw = new_plane(w_scales, "w_sc_raw")
        w0_sc_raw = new_plane(w0_scales, "w0_sc_raw")
        ws_sc = new_plane(ws_scales, "ws_sc")
        wb_sc = new_plane(wb_scales, "wb_sc")

        nc.gpsimd.memset(xt_sc[:].bitcast(I32), 0)
        nc.vector.memset(xo_sc[:].bitcast(I32), 0)
        load_low(w_sc_raw, w_scales, nc.gpsimd)
        load_high(w0_sc_raw, w0_scales, nc.gpsimd)
        l1 = load_list(offs, "l1")
        load_quadrants(xt_sc, xt_scales, nc.scalar)
        w_raw = load_weight(w_words, "w_raw")
        xt = load_table(xt_words, "xt")
        load_high(w_sc_raw, w_scales, nc.sync)
        xo = load_table(xo_words, "xo")
        l2 = load_list(offs2, "l2")
        load_low(w0_sc_raw, w0_scales, nc.sync)
        w0_raw = load_weight(w0_words, "w0_raw")
        load_quadrants(xo_sc, xo_scales, nc.sync)
        l6 = load_list(offs6, "l6")
        l3 = load_list(offs3, "l3")
        l4 = load_list(offs4, "l4")
        l5 = load_list(offs5, "l5")
        ws = load_weight(ws_words, "ws")
        load_high(ws_sc, ws_scales, nc.sync)
        load_low(ws_sc, ws_scales, nc.sync)
        wb = load_weight(wb_words, "wb")
        load_high(wb_sc, wb_scales, nc.sync)
        load_low(wb_sc, wb_scales, nc.sync)

        boards = [sb.tile([P, C], F32, name="board%d" % t) for t in range(PACK)]
        for t, board in enumerate(boards):
            (nc.gpsimd if t < 2 else nc.vector).memset(board[:], 0.0)

        def deal_words(raw, name):
            words = sb.tile([P, 2 * R], U8, name=name, align_bytes=ALIGN)
            nc.scalar.copy(
                words[:].bitcast(U16).rearrange("p (t m) -> p t m", t=PACK),
                raw[:].bitcast(U16).rearrange("p (m t) -> p t m", t=PACK),
            )
            return words

        def deal_scales(raw, name):
            scales = sb.tile([P, R], U8, name=name, align_bytes=ALIGN)
            nc.vector.tensor_copy(
                scales[:].rearrange("p (t m) -> p t m", t=PACK),
                raw[:].rearrange("p (m t) -> p t m", t=PACK),
            )
            return scales

        def gather(window, offsets, name, tag=None):
            picked = sb.tile([P, P], window.dtype, name=name, tag=tag or name, align_bytes=ALIGN)
            nc.vector.tensor_copy(picked[:], window[:].indirect(offsets))
            return picked

        def half(offsets, h):
            return offsets[:, HALF_COLS * h : HALF_COLS * (h + 1)]

        def mx(acc, weight, weight_sc, block, moving, moving_sc, fmt, start, stop):
            nc.tensor.matmul_mx(
                acc,
                lhsT=weight[:, 2 * P * block : 2 * P * (block + 1)].bitcast(E2M1),
                lhsT_scale=weight_sc[:, P * block : P * (block + 1)],
                rhs=moving[:].bitcast(fmt),
                rhs_scale=moving_sc[:],
                start=start,
                stop=stop,
            )

        toks = [(gather(xt, half(l1, 0), "tok0"), gather(xt_sc, half(l1, 0), "tok0_sc"))]
        w_sc = deal_scales(w_sc_raw, "w_sc")
        toks.append((gather(xt, half(l1, 1), "tok1"), gather(xt_sc, half(l1, 1), "tok1_sc")))
        w = deal_words(w_raw, "w")
        w0 = deal_words(w0_raw, "w0")
        note0 = gather(xo, half(l2, 0), "note0")
        w0_sc = deal_scales(w0_sc_raw, "w0_sc")
        notes = [(note0, gather(xo_sc, half(l2, 0), "note0_sc"))]
        notes.append((gather(xo, half(l2, 1), "note1"), gather(xo_sc, half(l2, 1), "note1_sc")))

        parts = [(0, 0), (0, 1), (1, 1), (1, 0)]
        accs = {part: psum.tile([P, 2, HALF], F32, name="acc%d%d" % part) for part in parts}
        for h, pair in parts:
            for u in range(2):
                mx(accs[h, pair][:, u, :], w, w_sc, 2 * pair + u, *toks[h], E5M2, u == 0, False)
        for h, pair in parts:
            for u in range(2):
                mx(accs[h, pair][:, u, :], w0, w0_sc, 2 * pair + u, *notes[h], E4M3, False, u == 1)

        short = (gather(xt, l6[:], "short", "tok1"), gather(xt_sc, l6[:], "short_sc", "tok1_sc"))
        ys = [psum.tile([P, O], F32, name="y%d" % block) for block in range(N // P)]
        for block in range(N // P):
            mx(ys[block][:], ws, ws_sc, block, *short, E5M2, True, False)

        for h, pair in [(0, 0), (1, 1), (0, 1), (1, 0)]:
            a = sb.tile([P, 2, HALF], F32, name="a%d%d" % (h, pair))
            if h == 0:
                nc.scalar.copy(a[:], accs[h, pair][:])
            else:
                nc.vector.tensor_copy(a[:], accs[h, pair][:])
            for u in range(2):
                columns = boards[2 * pair + u][:].indirect(half(l3, h))
                if h == 0:
                    nc.scalar.activation(columns, a[:, u, :], COPY)
                else:
                    nc.vector.tensor_copy(columns, a[:, u, :])

        first = sb.tile([P, PACK, O], F32, name="first")
        second = sb.tile([P, PACK, O], F32, name="second")
        for t in (2, 3, 0, 1):
            for picked, offsets in ((first, l4), (second, l5)):
                columns = boards[t][:].indirect(offsets[:])
                if t >= 2:
                    nc.scalar.activation(picked[:, t, :], columns, COPY)
                else:
                    nc.vector.tensor_copy(picked[:, t, :], columns)

        hid = sb.tile([P, O * PACK], BF16, name="hid", align_bytes=ALIGN)
        nc.vector.tensor_tensor(
            hid[:].rearrange("p (c i t) -> p c t i", i=4, t=PACK),
            first[:].rearrange("p t (c i) -> p c t i", i=4),
            second[:].rearrange("p t (c i) -> p c t i", i=4),
            MAX,
        )
        hq = sb.tile([P, O], U32, name="hq", align_bytes=ALIGN)
        hq_sc = sb.tile([P, O], U8, name="hq_sc", align_bytes=ALIGN)
        nc.vector.quantize_mx(out=hq[:].bitcast(E4M3), scales=hq_sc[:], in_=hid[:])

        for block in range(N // P):
            mx(ys[block][:], wb, wb_sc, block, hq, hq_sc, E4M3, False, True)
            res = sb.tile([P, O], F32, name="res%d" % block)
            rows = out[P * block : P * (block + 1), :]
            if block == 0:
                nc.scalar.copy(res[:], ys[block][:])
                nc.scalar.dma_start(rows, res[:])
            else:
                nc.vector.tensor_copy(res[:], ys[block][:])
                nc.sync.dma_start(rows, res[:])
